import numpy as np
import ml_dtypes


def mxq(x, axis, fmt="e4m3"):
    dtype, down = {"e4m3": (ml_dtypes.float8_e4m3fn, 7), "e5m2": (ml_dtypes.float8_e5m2, 14)}[fmt]
    v = np.moveaxis(np.asarray(x, np.float32).astype(ml_dtypes.bfloat16).astype(np.float64), axis, -1)
    blocks = v.reshape(v.shape[:-1] + (-1, 32))
    amax = np.abs(blocks).max(-1, keepdims=True)
    byte = np.maximum(np.where(amax > 0, np.frexp(amax)[1] - 1 + 127, 0) - down, 1)
    scale = np.exp2(byte - 127.0)
    codes = (blocks / scale).astype(np.float32).astype(dtype).astype(np.float64)
    return np.moveaxis((codes * scale).reshape(v.shape), -1, axis)


WIDE = False


def mx_kscale(k):
    if not WIDE:
        return np.ones(k)
    levels = np.array([10, -10, 5, -5, 0])
    if k % 512:
        return np.exp2(np.random.permutation(np.resize(levels, k // 32))).repeat(32)
    a = np.empty((k // 512, 16))
    for p in range(k // 512):
        a[p, :8] = np.random.permutation(np.resize(levels, 8))
        for g in range(8):
            far = levels[np.abs(levels - a[p, g]) >= 10]
            a[p, g + 8] = far[np.random.randint(len(far))]
    return np.exp2(a.ravel()).repeat(32)


BF16 = ml_dtypes.bfloat16


def bf(x):
    return np.asarray(x, np.float32).astype(BF16)


def f64(x):
    return np.asarray(x).astype(np.float64)


E2M1 = np.array([0.0, 0.5, 1.0, 1.5, 2.0, 3.0, 4.0, 6.0, -0.0, -0.5, -1.0, -1.5, -2.0, -3.0, -4.0, -6.0])


def pack_weight(w, fmt):
    k, n = w.shape
    w = f64(bf(w)).reshape(k // 32, 32, n)
    amax = np.abs(w).max(1)
    if fmt == "e4m3":
        byte = np.frexp(amax)[1] - 1 + 127 - 7
    else:
        mant, ex = np.frexp(amax / 6.0)
        byte = np.where(mant > 0.5, ex, ex - 1) + 127
    byte = np.clip(np.where(amax > 0, byte, 1), 1, 254)
    scaled = (w * np.exp2(127.0 - byte)[:, None, :]).reshape(k, n).astype(np.float32)
    by_word = np.ascontiguousarray(scaled.reshape(k // 512, 128, 4, n).transpose(0, 1, 3, 2))
    if fmt == "e4m3":
        words = by_word.astype(ml_dtypes.float8_e4m3fn).view(np.uint8)
    else:
        c = by_word.astype(ml_dtypes.float4_e2m1fn).view(np.uint8) & 0xF
        words = c[..., 0::2] | (c[..., 1::2] << 4)
    return np.ascontiguousarray(words), np.ascontiguousarray(byte.astype(np.uint8).reshape(k // 512, 16, n))


def unpack_weight(words, scales, fmt):
    g, p, n, _ = words.shape
    if fmt == "e4m3":
        vals = np.ascontiguousarray(words).view(ml_dtypes.float8_e4m3fn).astype(np.float64)
    else:
        nib = np.empty((g, p, n, 4), np.uint8)
        nib[..., 0::2] = words & 0xF
        nib[..., 1::2] = words >> 4
        vals = E2M1[nib]
    vals = vals * np.repeat(np.exp2(scales.astype(np.float64) - 127.0), 8, axis=1)[..., None]
    return vals.transpose(0, 1, 3, 2).reshape(g * 512, n)
def pack4(w):
    words, scales = pack_weight(w, "e2m1")
    return words.reshape(words.shape[0], 128, -1), scales


def unpack4(words, scales):
    return unpack_weight(words.reshape(words.shape[0], 128, -1, 2), scales, "e2m1")


def planes(Y):
    n, m = Y.shape
    b = f64(bf(Y)).reshape(n // 32, 32, m)
    amax = np.abs(b).max(1)
    byte = np.clip(np.where(amax > 0, np.frexp(amax)[1] - 1 + 127 - 7, 1), 1, 254)
    codes = (b * np.exp2(127.0 - byte)[:, None, :]).reshape(n, m).astype(np.float32).astype(ml_dtypes.float8_e4m3fn).view(np.uint8)
    words = codes.reshape(n // 512, 128, 4, m).transpose(0, 1, 3, 2)
    return np.ascontiguousarray(words), np.ascontiguousarray(byte.astype(np.uint8).reshape(n // 512, 16, m))


A, Z = 1536, 512

SHARE = 0.33
SPREAD = 0.8


def setup_inputs():
    rn = np.random.randn
    s1, t2, s3 = mx_kscale(A), mx_kscale(Z), mx_kscale(A)
    size = np.exp(SPREAD * rn(A))
    dev = rn(A, Z) * t2[None, :] / s1[:, None]
    move = SHARE * rn(A, A) / np.sqrt(A) * s1[:, None] / s3[None, :]
    shift = SHARE * rn(Z, Z) / np.sqrt(Z) / t2[:, None] * t2[None, :]
    carry = rn(A, A) / np.sqrt(A) * s3[:, None] * size[None, :]
    stay = (1 + 0.1 * rn(A)) * s1 / s3
    rate = (1 + 0.1 * rn(Z)) / t2
    entry = 0.3 * rn(A, Z) * size[:, None]
    move_words, move_scales = pack4(move)
    return {"dev": bf(dev), "move_words": move_words, "move_scales": move_scales,
            "stay": bf(stay), "shift": bf(shift), "carry": bf(carry),
            "rate": bf(rate), "entry": bf(entry)}


def reference(dev, move_words, move_scales, stay, shift, carry, rate, entry):
    X = f64(dev)
    G = unpack4(move_words, move_scales)
    P = G.T @ mxq(X, 0, "e4m3")
    D1 = f64(stay)[:, None] * X + P
    D2 = D1 + (mxq(D1, 1, "e4m3") @ mxq(f64(shift), 0, "e4m3"))
    C = mxq(f64(carry), 0, "e4m3")
    y = (C.T @ mxq(D2, 0, "e4m3")) * f64(rate)[None, :] + f64(entry)
    Y = y.reshape(A, Z)
    words, scales = planes(Y)
    return y, words, scales

from contextlib import ExitStack

import concourse.mybir as mybir
from concourse.masks import make_identity

A, Z = 1536, 512
P = 128
GROUP = 512
GROUPS = A // GROUP
PSUM_BANKS = 8
WEAVE_BUFFERS = 4
FLOPS = 2 * A * A * Z * 2 + 2 * A * Z * Z

F32 = mybir.dt.float32
BF16 = mybir.dt.bfloat16
U32 = mybir.dt.uint32
I32 = mybir.dt.int32
U8 = mybir.dt.uint8
FP8X4 = mybir.dt.float8_e4m3fn_x4
FP4X4 = mybir.dt.float4_e2m1fn_x4
ADD = mybir.AluOpType.add
MULT = mybir.AluOpType.mult
COPY = mybir.ActivationFunctionType.Copy

LOADS = """
dev_0 words_0 scales_02 dev_1 dev_2 stay shift words_1 dev_mid_0 carry_003 dev_mid_1 words_2 scales_23 carry_103
dev_mid_2 carry_203
"""
ENTRY_ORDER = (0, 2, 1)

STEPS = """
weave_x_001:s weave_x_034:v weave_x_012:v weave_x_023:s weave_x_101:s sort_words_0 sort_scales_0 quant_x_0
mm1_030 weave_x_134:s mm1_010 weave_x_123:v sort_scales_1 mm1_020 weave_x_112:v mm1_000 weave_x_201:v
weave_x_213:s quant_x_1 mm1_011 mm1_031 weave_x_234:v mm1_021 quant_x_2 weave_r_04:s mm1_001 sort_words_1
mm1_022 mm1_032 mm1_012 make_d1_02 make_d1_03 mm1_002 make_d1_00 mm1_120 make_d1_01 quant_r mm1_130 turn_d1_02
turn_d1_03 mm1_110 turn_d1_00 turn_d1_01 round_d1_02 round_d1_03 mm1_111 mm1_112 quant_d1_01 round_d1_00 mm1_131
round_d1_01 weave_c_0002:v quant_d1_00 mm1_121 make_d1_11 mm1_100 mm1_132 mm1_122 weave_c_0102:s mm2_02 mm2_01
make_d1_13 weave_c_0024:s mm1_101 make_d1_12 mm1_102 mm2_03 turn_d1_11 sort_words_2 sort_scales_2 make_d1_10
turn_d1_12 weave_c_0124:s round_d1_12 round_d1_11 mm2_00 turn_d1_13 quant_c_00 turn_d1_10 make_d2_02 mm1_210
make_d2_01 mm1_230 mm1_220 mm1_211 mm1_212 mm1_221 make_d2_03 round_d1_10 make_d2_00 round_d1_13 quant_d1_10
weave_c_1102:s mm1_200 mm1_201 weave_c_1004:s mm1_202 mm1_231 mm1_232 quant_d1_11 mm1_222 weave_c_0202:g
quant_c_01 quant_d2_01 make_d1_21 mm2_12 make_d1_22 mm3_030 mm2_11 turn_d1_21 make_d1_20 mm2_10 turn_d1_22
turn_d1_20 make_d1_23 round_d1_21 round_d1_22 turn_d1_23 quant_d2_00 quant_c_10 round_d1_23 make_d2_12 mm3_110
make_d2_10 round_d1_20 mm2_13 weave_c_1124:s make_d2_11 mm3_000 make_d2_13 quant_d1_20 quant_d1_21 quant_d2_10
quant_d2_11 mm3_120 weave_c_2102:s mm3_010 mm2_22 mm2_20 mm2_23 mm3_031 quant_c_11 mm3_111 mm3_001 make_d2_20
mm2_21 make_d2_23 weave_c_2002:s make_d2_22 mm3_100 make_d2_21 mm3_011 weave_c_2024:g quant_c_20 mm3_130
quant_d2_20 mm3_101 mm3_020 mm3_021 mm3_131 weave_c_2124:s mm3_002 quant_d2_21 mm3_012 mm3_022 mm3_121 mm3_032
quant_c_21 weave_c_0224:s mm3_112 mm3_122 quant_c_02 scale_y_00 mm3_132 weave_c_2202:g scale_y_01 scale_y_03
weave_c_1204:v mm3_210 scale_y_02 mm3_102 mm3_200 scale_y_11 weave_c_2224:v quant_c_12 turn_y_00 turn_y_02
turn_y_01 quant_c_22 make_y_00 scale_y_10 mm3_201 mm3_211 mm3_202 scale_y_12 scale_y_13 mm3_212 scale_y_20
turn_y_03 turn_y_11 turn_y_10 turn_y_12 make_y_02 make_y_01 mm3_230 store_y_00 make_y_03 make_y_10 store_y_02
mm3_231 mm3_232 scale_y_21 mm3_220 store_y_01 mm3_221 make_y_12 store_y_03 weave_y_001:v weave_y_012:g make_y_11
weave_y_024:s store_y_10 store_y_12 quant_y_00 store_y_11 quant_y_01 scale_y_23 mm3_222 turn_y_13 make_y_13
scale_y_22 turn_y_22 store_codes_002 weave_y_101:g weave_y_134:g turn_y_20 make_y_22 make_y_20 weave_y_113:s
store_y_13 turn_y_21 store_y_22 turn_y_23 store_y_20 make_y_21 store_y_21 make_y_23 quant_y_10 quant_y_11
weave_y_201:v weave_y_213:s weave_y_234:v store_y_23 store_codes_102 quant_y_20 store_codes_201 quant_y_21
store_codes_212
"""


def parse(item):
    pieces = item.split(":")
    words = pieces[0].split("_")
    if words[-1][0] in "0123456789":
        return "_".join(words[:-1]), [int(c) for c in words[-1]] + pieces[1:]
    return pieces[0], pieces[1:]


def tile_wealth_income_push_k1_kernel(
    tc, dev, move_words, move_scales, stay, shift, carry, rate, entry, out_0, out_1, out_2
):
    nc = tc.nc
    with ExitStack() as ctx:
        keep = ctx.enter_context(tc.tile_pool(name="keep", bufs=1))
        psum = ctx.enter_context(tc.psum_pool(name="psum", bufs=1))
        ctx.enter_context(tc.manual_schedule())

        def kept(name, shape, dtype):
            return keep.tile(shape, dtype, name=name, align_bytes=64)

        def per_group(name, shape, dtype):
            return [kept(name + str(g), shape, dtype) for g in range(GROUPS)]

        ident = kept("ident", [P, P], F32)
        stay_runs = kept("stay_runs", [P, GROUPS, 16], BF16)
        rate_bf = kept("rate_bf", [P, 4], BF16)
        rate_col = kept("rate_col", [P, 4], F32)
        x_plain = per_group("x_plain", [P, 4, Z], BF16)
        x_mid = per_group("x_mid", [P, 4, Z], BF16)
        x_codes = per_group("x_codes", [P, Z], U32)
        x_scales = per_group("x_scales", [P, Z], U8)
        words_raw = per_group("words_raw", [P, GROUPS, 2 * GROUP], U8)
        g_words = per_group("g_words", [P, GROUPS, 2 * GROUP], U8)
        g_scales = per_group("g_scales", [P, GROUPS, GROUP], U8)
        r_plain = kept("r_plain", [P, 4, Z], BF16)
        r_codes = kept("r_codes", [P, Z], U32)
        r_scales = kept("r_scales", [P, Z], U8)
        c_codes = per_group("c_codes", [P, A], U32)
        c_scales = per_group("c_scales", [P, A], U8)
        d1 = per_group("d1", [P, 4, Z], F32)
        d1_bf = per_group("d1_bf", [P, 4, GROUP], BF16)
        d1_codes = per_group("d1_codes", [P, GROUP], U32)
        d1_scales = per_group("d1_scales", [P, GROUP], U8)
        d2_bf = per_group("d2_bf", [P, 4, GROUP], BF16)
        d2_codes = per_group("d2_codes", [P, Z], U32)
        d2_scales = per_group("d2_scales", [P, Z], U8)
        y_codes = per_group("y_codes", [P, Z], U32)
        y_scales = kept("y_scales", [P, GROUPS, Z], U8)
        scales_raw, c_mid, entry_plain, scaled, y = {}, {}, {}, {}, {}

        free_banks = list(range(PSUM_BANKS))
        free_buffers = list(range(WEAVE_BUFFERS))
        banks, woven = {}, {}

        def take_bank(key):
            number = free_banks[0]
            free_banks.remove(number)
            banks[key] = (psum.tile([P, 512], F32, name="bank" + str(number)), number)

        def leave_bank(key):
            free_banks.append(banks[key][1])

        def weave_buffer(key):
            if key not in woven:
                number = free_buffers[0]
                free_buffers.remove(number)
                woven[key] = (kept("woven" + str(number), [P, 4 * GROUP], BF16), number)
            return woven[key][0]

        def leave_buffer(key):
            free_buffers.append(woven[key][1])

        def span(i, width, count=1):
            return slice(i * width, (i + count) * width)

        def load_plain(dst, rows):
            nc.sync.dma_start(out=dst[:], in_=rows.rearrange("(p t) z -> p t z", t=4))

        def load_mid(dst, rows):
            view = rows.rearrange("(q t s) n -> s q t n", t=4, s=4)
            for s in range(4):
                nc.sync.dma_start(out=dst[s:P:4], in_=view[s])

        def load_dev(g):
            load_plain(x_plain[g], dev[span(g, GROUP), :])

        def load_dev_mid(g):
            load_mid(x_mid[g], dev[span(g, GROUP), :])

        def load_shift():
            load_plain(r_plain, shift)

        def load_stay():
            runs = stay.rearrange("(g q e) -> q g e", g=GROUPS, e=16)
            for s in range(4):
                nc.sync.dma_start(out=stay_runs[s:P:4, :, 0:13], in_=runs[:, :, s : s + 13])

        def load_words(g):
            src = move_words.rearrange("k p n -> p k n")[:, :, span(g, 2 * GROUP)]
            nc.sync.dma_start(out=words_raw[g][:].bitcast(I32), in_=src.bitcast(I32))

        def load_scales(lo, hi):
            whole = kept("scales_raw" + str(lo), [P, GROUPS, GROUP * (hi - lo)], U8)
            nc.vector.memset(whole[:].rearrange("p k n -> p (k n)").bitcast(I32), 0)
            src = move_scales.rearrange("k q n -> q k n")[:, :, span(lo, GROUP, hi - lo)]
            for r in range(4):
                nc.sync.dma_start(out=whole[r:P:32].bitcast(I32), in_=src[r:16:4].bitcast(I32))
            for g in range(lo, hi):
                scales_raw[g] = whole[:, :, span(g - lo, GROUP)]

        def load_carry(k, lo, hi):
            whole = kept("carry" + str(k) + str(lo), [P, 4, GROUP * (hi - lo)], BF16)
            load_mid(whole, carry[span(k, GROUP), span(lo, GROUP, hi - lo)])
            for g in range(lo, hi):
                c_mid[k, g] = whole[:, :, span(g - lo, GROUP)]

        def load_rest():
            for g in ENTRY_ORDER:
                entry_plain[g] = kept("x_plain" + str(g), [P, 4, Z], BF16)
                load_plain(entry_plain[g], entry[span(g, GROUP), :])
            nc.sync.dma_start(out=rate_bf[:], in_=rate.rearrange("(m u) -> m u", u=4))

        scalar_started = []

        def weave(engine, key, src, lo, hi):
            dst = weave_buffer(key)[:, span(lo, 4 * P, hi - lo)]
            src = src[:, :, span(lo, P, hi - lo)]
            if engine == "g":
                nc.gpsimd.tensor_scalar(
                    out=dst.rearrange("p (c t) -> p c t", t=4),
                    in0=src.rearrange("p t c -> p c t"),
                    scalar1=1.0,
                    scalar2=0.0,
                    op0=MULT,
                    op1=ADD,
                )
                return
            dst = dst.rearrange("p (c i t) -> p c t i", i=4, t=4)
            src = src.rearrange("p t (c i) -> p c t i", i=4)
            if engine == "v":
                nc.vector.tensor_copy(out=dst, in_=src)
            elif scalar_started:
                nc.scalar.copy(out=dst, in_=src)
            else:
                scalar_started.append(True)
                nc.scalar.activation(out=dst, in_=src, func=COPY)

        def weave_x(k, lo, hi, engine):
            weave(engine, ("x", k), x_plain[k][:], lo, hi)

        def weave_c(k, g, lo, hi, engine):
            weave(engine, ("c", k, g), c_mid[k, g], lo, hi)

        def weave_y(g, lo, hi, engine):
            weave(engine, ("y", g), y[g][:], lo, hi)

        def weave_r(lo, hi, engine):
            dst = weave_buffer("r")[:].rearrange("p (u a b t) -> p a u b t", u=4, b=2, t=4)[:, :, lo:hi]
            src = r_plain[:].rearrange("p t (a b u) -> p a u b t", b=2, u=4)[:, :, lo:hi]
            if engine == "v":
                nc.vector.tensor_copy(out=dst, in_=src)
            else:
                nc.scalar.copy(out=dst, in_=src)

        def quantize(codes, scales, src):
            nc.vector.quantize_mx(out=codes.bitcast(FP8X4), scales=scales, in_=src)

        x_done = []

        def quant_x(k):
            quantize(x_codes[k][:], x_scales[k][:], weave_buffer(("x", k))[:])
            leave_buffer(("x", k))
            x_done.append(k)
            if len(x_done) == GROUPS:
                load_rest()

        def quant_r():
            quantize(r_codes[:], r_scales[:], weave_buffer("r")[:])
            leave_buffer("r")

        def quant_c(k, g):
            quantize(c_codes[k][:, span(g, GROUP)], c_scales[k][:, span(g, GROUP)], weave_buffer(("c", k, g))[:])
            leave_buffer(("c", k, g))

        def quant_d1(g, half):
            src = d1_bf[g][:, span(half, 2), :].rearrange("p t c -> p (t c)")
            quantize(d1_codes[g][:, span(half, 256)], d1_scales[g][:, span(half, 256)], src)

        def quant_d2(g, half):
            src = d2_bf[g][:, span(half, 2), :].rearrange("p u c -> p (u c)")
            quantize(d2_codes[g][:, span(half, 256)], d2_scales[g][:, span(half, 256)], src)

        def quant_y(g, half):
            src = weave_buffer(("y", g))[:, span(half, 1024)]
            quantize(y_codes[g][:, span(half, 256)], y_scales[:, g, span(half, 256)], src)
            if half == 1:
                leave_buffer(("y", g))

        def sort_words(g):
            nc.vector.tensor_copy(
                out=g_words[g][:].bitcast(I32).rearrange("p k (t q w) -> p t k q w", t=4, w=2),
                in_=words_raw[g][:].bitcast(I32).rearrange("p k (q t w) -> p t k q w", t=4, w=2),
            )

        def sort_scales(g):
            nc.vector.tensor_copy(
                out=g_scales[g][:].bitcast(I32).rearrange("p k (t a i) -> p a k t i", t=4, i=4),
                in_=scales_raw[g].bitcast(I32).rearrange("p k (a i t) -> p a k t i", t=4, i=4),
            )

        def mm1(g, t, k):
            if k == 0:
                take_bank(("mm1", g, t))
            nc.tensor.matmul_mx(
                out=banks["mm1", g, t][0][:],
                lhsT=g_words[g][:, k, span(t, 2 * P)].bitcast(FP4X4),
                lhsT_scale=g_scales[g][:, k, span(t, P)],
                rhs=x_codes[k][:].bitcast(FP8X4),
                rhs_scale=x_scales[k][:],
                start=(k == 0),
                stop=(k == GROUPS - 1),
            )

        def make_d1(g, t):
            nc.vector.scalar_tensor_tensor(
                out=d1[g][:, t, :].rearrange("p (u m) -> p u m", u=4),
                in0=x_mid[g][:, t, :].rearrange("p (m u) -> p u m", u=4),
                scalar=stay_runs[:, g, 4 * t : 4 * t + 1],
                in1=banks["mm1", g, t][0][:].rearrange("p (m u) -> p u m", u=4),
                op0=MULT,
                op1=ADD,
            )
            leave_bank(("mm1", g, t))

        def turn_d1(g, t):
            take_bank(("turn_d1", g, t))
            for u in range(4):
                nc.tensor.transpose(banks["turn_d1", g, t][0][:, span(u, P)], d1[g][:, t, span(u, P)], ident[:])

        def round_d1(g, t):
            nc.scalar.copy(
                out=d1_bf[g][:, t, :].rearrange("p (m u) -> p m u", u=4),
                in_=banks["turn_d1", g, t][0][:].rearrange("p (u m) -> p m u", u=4),
            )
            leave_bank(("turn_d1", g, t))

        def mm2(g, u):
            take_bank(("mm2", g, u))
            for t in range(4):
                nc.tensor.matmul_mx(
                    out=banks["mm2", g, u][0][:, span(t, P)],
                    lhsT=d1_codes[g][:, span(t, P)].bitcast(FP8X4),
                    lhsT_scale=d1_scales[g][:, span(t, P)],
                    rhs=r_codes[:, span(u, P)].bitcast(FP8X4),
                    rhs_scale=r_scales[:, span(u, P)],
                    start=True,
                    stop=True,
                )

        def make_d2(g, u):
            nc.vector.tensor_tensor(
                out=d2_bf[g][:, u, :].rearrange("p (a i t) -> p a t i", i=2, t=4),
                in0=banks["mm2", g, u][0][:].rearrange("p (t a i) -> p a t i", i=2, t=4),
                in1=d1[g][:, :, span(u, P)].rearrange("p t (a i) -> p a t i", i=2),
                op=ADD,
            )
            leave_bank(("mm2", g, u))

        def mm3(g, u, k):
            if k == 0:
                take_bank(("mm3", g, u))
            nc.tensor.matmul_mx(
                out=banks["mm3", g, u][0][:],
                lhsT=d2_codes[k][:, span(u, P)].bitcast(FP8X4),
                lhsT_scale=d2_scales[k][:, span(u, P)],
                rhs=c_codes[k][:, span(g, GROUP)].bitcast(FP8X4),
                rhs_scale=c_scales[k][:, span(g, GROUP)],
                start=(k == 0),
                stop=(k == GROUPS - 1),
            )

        def scale_y(g, u):
            if not scaled:
                nc.scalar.activation(out=rate_col[:], in_=rate_bf[:], func=COPY)
            if (g, u // 2) not in scaled:
                scaled[g, u // 2] = kept(("x_mid", "d1_bf")[u // 2] + str(g), [P, 2, GROUP], F32)
            nc.scalar.activation(
                out=scaled[g, u // 2][:, u % 2, :].rearrange("m (t p) -> m t p", t=4),
                in_=banks["mm3", g, u][0][:].rearrange("m (p t) -> m t p", t=4),
                func=COPY,
                scale=rate_col[:, u : u + 1],
            )
            leave_bank(("mm3", g, u))

        def turn_y(g, t):
            take_bank(("turn_y", g, t))
            for u in range(4):
                nc.tensor.transpose(
                    banks["turn_y", g, t][0][:, span(u, P)], scaled[g, u // 2][:, u % 2, span(t, P)], ident[:]
                )

        def make_y(g, t):
            if g not in y:
                y[g] = kept("d1" + str(g), [P, 4, Z], F32)
            nc.vector.tensor_tensor(
                out=y[g][:, t, :].rearrange("p (m u) -> p m u", u=4),
                in0=banks["turn_y", g, t][0][:].rearrange("p (u m) -> p m u", u=4),
                in1=entry_plain[g][:, t, :].rearrange("p (m u) -> p m u", u=4),
                op=ADD,
            )
            leave_bank(("turn_y", g, t))

        def store_y(g, t):
            rows = out_0[span(g, GROUP), :].rearrange("(p t) z -> p t z", t=4)
            nc.sync.dma_start(out=rows[:, t, :], in_=y[g][:, t, :])

        def store_codes(g, lo, hi):
            cols = span(lo, 256, hi - lo)
            words = out_1[g].rearrange("p m t -> p (m t)").bitcast(I32)
            nc.sync.dma_start(out=words[:, cols], in_=y_codes[g][:, cols].bitcast(I32))

        def store_scales():
            rows = out_2.rearrange("g q m -> q g m")
            for r in range(4):
                queue = nc.scalar if r % 2 else nc.sync
                queue.dma_start(out=rows[r:16:4].bitcast(I32), in_=y_scales[r:P:32].bitcast(I32))

        loads = {
            "dev": load_dev,
            "dev_mid": load_dev_mid,
            "shift": load_shift,
            "stay": load_stay,
            "words": load_words,
            "scales": load_scales,
            "carry": load_carry,
        }
        steps = {
            "weave_x": weave_x,
            "weave_r": weave_r,
            "weave_c": weave_c,
            "weave_y": weave_y,
            "quant_x": quant_x,
            "quant_r": quant_r,
            "quant_c": quant_c,
            "quant_d1": quant_d1,
            "quant_d2": quant_d2,
            "quant_y": quant_y,
            "sort_words": sort_words,
            "sort_scales": sort_scales,
            "mm1": mm1,
            "make_d1": make_d1,
            "turn_d1": turn_d1,
            "round_d1": round_d1,
            "mm2": mm2,
            "make_d2": make_d2,
            "mm3": mm3,
            "scale_y": scale_y,
            "turn_y": turn_y,
            "make_y": make_y,
            "store_y": store_y,
            "store_codes": store_codes,
        }

        make_identity(nc, ident[:])
        for item in LOADS.split():
            name, args = parse(item)
            loads[name](*args)
        for item in STEPS.split():
            name, args = parse(item)
            steps[name](*args)
        store_scales()
